import numpy as np
import ml_dtypes


def mxq(x, axis, fmt="e4m3"):
    dtype, down = {"e4m3": (ml_dtypes.float8_e4m3fn, 7), "e5m2": (ml_dtypes.float8_e5m2, 14)}[fmt]
    v = np.moveaxis(np.asarray(x, np.float32).astype(ml_dtypes.bfloat16).astype(np.float64), axis, -1)
    blocks = v.reshape(v.shape[:-1] + (-1, 32))
    amax = np.abs(blocks).max(-1, keepdims=True)
    byte = np.maximum(np.where(amax > 0, np.frexp(amax)[1] - 1 + 127, 0) - down, 1)
    scale = np.exp2(byte - 127.0)
    codes = (blocks / scale).astype(np.float32).astype(dtype).astype(np.float64)
    return np.moveaxis((codes * scale).reshape(v.shape), -1, axis)


WIDE = False


def mx_kscale(k, group=512):
    if not WIDE:
        return np.ones(k)
    levels = np.array([10, -10, 5, -5, 0])
    if group != 512:
        return np.exp2(np.random.permutation(np.resize(levels, k // group))).repeat(group)
    if k % 512:
        return np.exp2(np.random.permutation(np.resize(levels, k // 32))).repeat(32)
    a = np.empty((k // 512, 16))
    for p in range(k // 512):
        a[p, :8] = np.random.permutation(np.resize(levels, 8))
        for g in range(8):
            far = levels[np.abs(levels - a[p, g]) >= 10]
            a[p, g + 8] = far[np.random.randint(len(far))]
    return np.exp2(a.ravel()).repeat(32)


def f64(x):
    return np.asarray(x).astype(np.float64)


def striped(idx):
    return np.tile(np.asarray(idx).reshape(-1, 16).T, (8, 1)).astype(np.uint16)


def unstriped(offs):
    return offs[:16].T.reshape(-1).astype(np.int64)


H, KV, D, NQ, N = 4, 1, 128, 512, 512
CAP = 2.0


def setup_inputs():
    n = np.random.standard_normal
    s = mx_kscale(D, 0)[:, None]
    u = mx_kscale(N)
    t = np.random.uniform(0.5, 2.0, N) * u
    v = n((KV, N, 128))
    return {
        "qT": (n((H, D, NQ)) * s * (0.70 / np.sqrt(D))).astype(np.float32),
        "kT": (n((KV, D, N)) / s).astype(np.float32),
        "t": t.reshape(N, 1).astype(np.float32),
        "v": (v / t[:, None]).astype(np.float32),
    }


def reference(qT, kT, t, v):
    a = np.repeat(mxq(f64(kT), 1, "e4m3"), H // KV, 0).transpose(0, 2, 1) @ mxq(f64(qT), 1, "e4m3")
    a = CAP * np.tanh(a / CAP)
    p = np.maximum(a, 0.0)
    w = p * f64(t)
    y = mxq(w, 1, "e4m3").transpose(0, 2, 1) @ np.repeat(mxq(f64(v), 1, "e4m3"), H // KV, 0)
    y = y / 16.0
    return y

@@ -1,0 +1,197 @@
+from contextlib import ExitStack
+
+import concourse.mybir as mybir
+
+H, D, NQ, N = 4, 128, 512, 512
+FLOPS = 2 * 2 * H * NQ * N * D
+
+F32 = mybir.dt.float32
+BF16 = mybir.dt.bfloat16
+U32 = mybir.dt.uint32
+U8 = mybir.dt.uint8
+FP8X4 = mybir.dt.float8_e4m3fn_x4
+ACT = mybir.ActivationFunctionType
+ALU = mybir.AluOpType
+
+P = 128
+PACK = 4
+ROWS = D // PACK
+W = 128
+CHUNKS = NQ // W
+UNITS = CHUNKS * H
+S_SPLIT = 40
+GROUPS = [(0, 1), (1, 2)] + [(u, u + 2) for u in range(2, UNITS - 2, 2)] + [(UNITS - 2, UNITS - 1), (UNITS - 1, UNITS)]
+LAG = 5
+
+
+def tile_rows_a_relu_cap_kernel(tc, qT, kT, t, v, out):
+    nc = tc.nc
+    with ExitStack() as ctx:
+        sb = ctx.enter_context(tc.tile_pool(name="sb", bufs=1))
+        ps = ctx.enter_context(tc.psum_pool(name="ps", bufs=1))
+
+        def tiles(name, count, shape, dtype):
+            return [sb.tile(shape, dtype, name="%s%d" % (name, i), align_bytes=64) for i in range(count)]
+
+        k_raw = tiles("k_raw", 2, [P, PACK, N // 2], F32)
+        q_raw = tiles("q_raw", CHUNKS, [P, PACK, W], F32)
+        v_raw = sb.tile([P, PACK, W], F32, align_bytes=64)
+        t_sb = sb.tile([P, PACK], F32, align_bytes=64)
+        k_bf = sb.tile([P, PACK, W, PACK], BF16, align_bytes=64)
+        q_bf = tiles("q_bf", CHUNKS, [P, W, PACK], BF16)
+        v_bf = sb.tile([P, W, PACK], BF16, align_bytes=64)
+        k_codes = tiles("k_codes", PACK, [P, W], U32)
+        k_scales = tiles("k_scales", PACK, [P, W], U8)
+        q_codes = tiles("q_codes", CHUNKS, [P, W], U32)
+        q_scales = tiles("q_scales", CHUNKS, [P, W], U8)
+        v_codes = sb.tile([P, W], U32, align_bytes=64)
+        v_scales = sb.tile([P, W], U8, align_bytes=64)
+        capped = sb.tile([P, UNITS * W, PACK], F32, align_bytes=64)
+        w_bf = sb.tile([P, UNITS * W, PACK], BF16, align_bytes=64)
+        w_codes = sb.tile([P, UNITS * W], U32, align_bytes=64)
+        w_scales = sb.tile([P, UNITS * W], U8, align_bytes=64)
+        res = tiles("res", CHUNKS, [P, H, W], F32)
+        warm_in = sb.tile([P, 1], F32, align_bytes=64)
+        warm_out = sb.tile([P, 1], F32, align_bytes=64)
+        s_bank = [ps.tile([P, PACK, W], F32, name="s_bank%d" % g) for g in range(H)]
+        y_bank = [ps.tile([P, H, W], F32, name="y_bank%d" % g) for g in range(4)]
+
+        k_view = kT[0].rearrange("(p j) n -> p j n", j=PACK)
+        q_view = qT.rearrange("h (p j) n -> (h p) j n", j=PACK)
+
+        def load_k(eng, half, g):
+            eng.dma_start(out=k_raw[half][ROWS * g : ROWS * (g + 1)], in_=k_view[:, :, 256 * half : 256 * (half + 1)])
+
+        def load_q(c):
+            nc.sync.dma_start(out=q_raw[c][:], in_=q_view[:, :, W * c : W * (c + 1)])
+
+        def deal_k(copy, s0, s1):
+            half = s0 // 64
+            src = k_raw[half][:].rearrange("p j (s r) -> p s j r", r=PACK)[:, s0 - 64 * half : s1 - 64 * half]
+            copy(out=k_bf[:, :, s0:s1, :].rearrange("p r s j -> p s j r"), in_=src)
+
+        def interleave(copy, dst, src):
+            copy(out=dst[:].rearrange("p (c i) j -> p c j i", i=4), in_=src[:].rearrange("p j (c i) -> p c j i", i=4))
+
+        def quantize(codes, scales, src):
+            nc.vector.quantize_mx(out=codes.bitcast(FP8X4), scales=scales, in_=src.rearrange("p c j -> p (c j)"))
+
+        def scores(u, r):
+            c, g = divmod(u, H)
+            rows = slice(ROWS * g, ROWS * (g + 1))
+            nc.tensor.matmul_mx(
+                out=s_bank[g][:, r, :],
+                lhsT=k_codes[r][rows, :].bitcast(FP8X4),
+                lhsT_scale=k_scales[r][rows, :],
+                rhs=q_codes[c][rows, :].bitcast(FP8X4),
+                rhs_scale=q_scales[c][rows, :],
+                start=True,
+                stop=True,
+            )
+
+        def y_slot(u):
+            c, g = divmod(u, H)
+            if c < CHUNKS - 1 or g < 2:
+                return y_bank[c]
+            return y_bank[g - 2]
+
+        def second(u):
+            g = u % H
+            nc.tensor.matmul_mx(
+                out=y_slot(u)[:, g, :],
+                lhsT=w_codes[:, W * u : W * (u + 1)].bitcast(FP8X4),
+                lhsT_scale=w_scales[:, W * u : W * (u + 1)],
+                rhs=v_codes[:].bitcast(FP8X4),
+                rhs_scale=v_scales[:],
+                start=True,
+                stop=True,
+            )
+
+        def store(c, g0, g1):
+            bank = y_slot(c * H + g0)
+            nc.scalar.activation(out=res[c][:, g0:g1, :], in_=bank[:, g0:g1, :], func=ACT.Copy, scale=0.125)
+            nc.sync.dma_start(
+                out=out[g0:g1, W * c : W * (c + 1), :].rearrange("h p e -> p h e"), in_=res[c][:, g0:g1, :]
+            )
+
+        with tc.manual_schedule():
+            load_q(0)
+            for half in range(2):
+                for g in range(2):
+                    load_k(nc.sync, half, g)
+                    load_k(nc.scalar, half, g + 2)
+            load_q(1)
+            nc.sync.dma_start(out=t_sb[:], in_=t.rearrange("(p j) o -> p (j o)", j=PACK))
+            nc.sync.dma_start(out=v_raw[:], in_=v[0].rearrange("(p j) e -> p j e", j=PACK))
+            load_q(2)
+            load_q(3)
+
+            nc.vector.memset(warm_in[:], 0.0)
+            nc.scalar.activation(out=warm_out[:], in_=warm_in[:], func=ACT.Tanh, scale=0.5)
+
+            interleave(nc.vector.tensor_copy, q_bf[0], q_raw[0])
+            quantize(q_codes[0][:], q_scales[0][:], q_bf[0][:])
+            for half in range(2):
+                s0 = 64 * half
+                deal_k(nc.vector.tensor_copy, s0, s0 + S_SPLIT)
+                deal_k(nc.scalar.copy, s0 + S_SPLIT, s0 + 64)
+                for r in range(PACK):
+                    quantize(k_codes[r][:, s0 : s0 + 64], k_scales[r][:, s0 : s0 + 64], k_bf[:, r, s0 : s0 + 64])
+            for r in range(PACK):
+                for g in range(H):
+                    scores(g, r)
+            interleave(nc.scalar.copy, q_bf[1], q_raw[1])
+            quantize(q_codes[1][:], q_scales[1][:], q_bf[1][:])
+            interleave(nc.vector.tensor_copy, v_bf, v_raw)
+            interleave(nc.vector.tensor_copy, q_bf[2], q_raw[2])
+            quantize(v_codes[:], v_scales[:], v_bf[:])
+
+            def weigh(u0, u1):
+                cols = slice(W * u0, W * u1)
+                t_rep = t_sb[:].unsqueeze(1).to_broadcast([P, W * (u1 - u0), PACK])
+                nc.vector.scalar_tensor_tensor(
+                    out=w_bf[:, cols], in0=capped[:, cols], scalar=0.0, in1=t_rep, op0=ALU.max, op1=ALU.mult
+                )
+
+            def quantize_w(u0, u1):
+                cols = slice(W * u0, W * u1)
+                quantize(w_codes[:, cols], w_scales[:, cols], w_bf[:, cols])
+
+            group_ending = {u1 - 1: i for i, (u0, u1) in enumerate(GROUPS)}
+            for s in range(UNITS + LAG):
+                if s < UNITS:
+                    nc.scalar.activation(
+                        out=capped[:, W * s : W * (s + 1)],
+                        in_=s_bank[s % H][:].rearrange("p r q -> p q r"),
+                        func=ACT.Tanh,
+                        scale=0.5,
+                    )
+                if s in (9, 13, 17):
+                    store((s - 9) // H, 0, H)
+                for r in range(2):
+                    if s + 4 < UNITS:
+                        scores(s + 4, r)
+                    if H <= s + 3 < UNITS:
+                        scores(s + 3, r + 2)
+                if s in group_ending:
+                    i = group_ending[s]
+                    weigh(*GROUPS[i])
+                    if i == 0:
+                        quantize(q_codes[2][:], q_scales[2][:], q_bf[2][:])
+                    elif i == 1:
+                        quantize_w(*GROUPS[0])
+                        interleave(nc.vector.tensor_copy, q_bf[3], q_raw[3])
+                        quantize_w(*GROUPS[1])
+                    elif i == 2:
+                        quantize(q_codes[3][:], q_scales[3][:], q_bf[3][:])
+                    else:
+                        quantize_w(*GROUPS[i - 1])
+                if s == UNITS - 1:
+                    quantize_w(*GROUPS[-1])
+                if s - LAG in group_ending:
+                    for u in range(*GROUPS[group_ending[s - LAG]]):
+                        second(u)
+                if s == 18:
+                    store(3, 0, 2)
+                if s >= 19:
+                    store(3, s - 17, s - 16)

@@ -19,9 +19,7 @@ ROWS = D // PACK
 W = 128
 CHUNKS = NQ // W
 UNITS = CHUNKS * H
-S_SPLIT = 40
 GROUPS = [(0, 1), (1, 2)] + [(u, u + 2) for u in range(2, UNITS - 2, 2)] + [(UNITS - 2, UNITS - 1), (UNITS - 1, UNITS)]
-LAG = 5
 
 
 def tile_rows_a_relu_cap_kernel(tc, qT, kT, t, v, out):
@@ -65,10 +63,11 @@ def tile_rows_a_relu_cap_kernel(tc, qT, kT, t, v, out):
         def load_q(c):
             nc.sync.dma_start(out=q_raw[c][:], in_=q_view[:, :, W * c : W * (c + 1)])
 
-        def deal_k(copy, s0, s1):
+        def deal_k(copy, s0, s1, r0):
             half = s0 // 64
-            src = k_raw[half][:].rearrange("p j (s r) -> p s j r", r=PACK)[:, s0 - 64 * half : s1 - 64 * half]
-            copy(out=k_bf[:, :, s0:s1, :].rearrange("p r s j -> p s j r"), in_=src)
+            src = k_raw[half][:].rearrange("p j (s r) -> p s j r", r=PACK)
+            src = src[:, s0 - 64 * half : s1 - 64 * half, :, r0 : r0 + 2]
+            copy(out=k_bf[:, r0 : r0 + 2, s0:s1, :].rearrange("p r s j -> p s j r"), in_=src)
 
         def interleave(copy, dst, src):
             copy(out=dst[:].rearrange("p (c i) j -> p c j i", i=4), in_=src[:].rearrange("p j (c i) -> p c j i", i=4))
@@ -115,13 +114,13 @@ def tile_rows_a_relu_cap_kernel(tc, qT, kT, t, v, out):
             )
 
         with tc.manual_schedule():
+            nc.gpsimd.dma_start(out=t_sb[:], in_=t.rearrange("(p j) o -> p (j o)", j=PACK))
             load_q(0)
             for half in range(2):
                 for g in range(2):
                     load_k(nc.sync, half, g)
                     load_k(nc.scalar, half, g + 2)
             load_q(1)
-            nc.sync.dma_start(out=t_sb[:], in_=t.rearrange("(p j) o -> p (j o)", j=PACK))
             nc.sync.dma_start(out=v_raw[:], in_=v[0].rearrange("(p j) e -> p j e", j=PACK))
             load_q(2)
             load_q(3)
@@ -133,18 +132,19 @@ def tile_rows_a_relu_cap_kernel(tc, qT, kT, t, v, out):
             quantize(q_codes[0][:], q_scales[0][:], q_bf[0][:])
             for half in range(2):
                 s0 = 64 * half
-                deal_k(nc.vector.tensor_copy, s0, s0 + S_SPLIT)
-                deal_k(nc.scalar.copy, s0 + S_SPLIT, s0 + 64)
+                deal_k(nc.vector.tensor_copy, s0, s0 + 64, 0)
+                deal_k(nc.vector.tensor_copy, s0, s0 + 32, 2)
+                deal_k(nc.scalar.copy, s0 + 32, s0 + 64, 2)
                 for r in range(PACK):
                     quantize(k_codes[r][:, s0 : s0 + 64], k_scales[r][:, s0 : s0 + 64], k_bf[:, r, s0 : s0 + 64])
-            for r in range(PACK):
-                for g in range(H):
+            for g in range(H):
+                for r in range(PACK):
                     scores(g, r)
             interleave(nc.scalar.copy, q_bf[1], q_raw[1])
-            quantize(q_codes[1][:], q_scales[1][:], q_bf[1][:])
             interleave(nc.vector.tensor_copy, v_bf, v_raw)
-            interleave(nc.vector.tensor_copy, q_bf[2], q_raw[2])
+            quantize(q_codes[1][:], q_scales[1][:], q_bf[1][:])
             quantize(v_codes[:], v_scales[:], v_bf[:])
+            interleave(nc.vector.tensor_copy, q_bf[2], q_raw[2])
 
             def weigh(u0, u1):
                 cols = slice(W * u0, W * u1)
@@ -158,7 +158,7 @@ def tile_rows_a_relu_cap_kernel(tc, qT, kT, t, v, out):
                 quantize(w_codes[:, cols], w_scales[:, cols], w_bf[:, cols])
 
             group_ending = {u1 - 1: i for i, (u0, u1) in enumerate(GROUPS)}
-            for s in range(UNITS + LAG):
+            for s in range(UNITS):
                 if s < UNITS:
                     nc.scalar.activation(
                         out=capped[:, W * s : W * (s + 1)],
@@ -166,13 +166,9 @@ def tile_rows_a_relu_cap_kernel(tc, qT, kT, t, v, out):
                         func=ACT.Tanh,
                         scale=0.5,
                     )
-                if s in (9, 13, 17):
-                    store((s - 9) // H, 0, H)
-                for r in range(2):
-                    if s + 4 < UNITS:
-                        scores(s + 4, r)
-                    if H <= s + 3 < UNITS:
-                        scores(s + 3, r + 2)
+                if s + H < UNITS:
+                    for r in range(PACK):
+                        scores(s + H, r)
                 if s in group_ending:
                     i = group_ending[s]
                     weigh(*GROUPS[i])
@@ -180,18 +176,20 @@ def tile_rows_a_relu_cap_kernel(tc, qT, kT, t, v, out):
                         quantize(q_codes[2][:], q_scales[2][:], q_bf[2][:])
                     elif i == 1:
                         quantize_w(*GROUPS[0])
-                        interleave(nc.vector.tensor_copy, q_bf[3], q_raw[3])
                         quantize_w(*GROUPS[1])
-                    elif i == 2:
-                        quantize(q_codes[3][:], q_scales[3][:], q_bf[3][:])
-                    else:
+                    elif i > 2:
                         quantize_w(*GROUPS[i - 1])
-                if s == UNITS - 1:
-                    quantize_w(*GROUPS[-1])
-                if s - LAG in group_ending:
-                    for u in range(*GROUPS[group_ending[s - LAG]]):
-                        second(u)
-                if s == 18:
-                    store(3, 0, 2)
-                if s >= 19:
-                    store(3, s - 17, s - 16)
+                if s == 7:
+                    interleave(nc.scalar.copy, q_bf[3], q_raw[3])
+                    quantize(q_codes[3][:], q_scales[3][:], q_bf[3][:])
+            quantize_w(*GROUPS[-1])
+            for u in range(UNITS):
+                second(u)
+                c, g = divmod(u, H)
+                if c < CHUNKS - 1:
+                    if g == H - 1:
+                        store(c, 0, H)
+                elif g == 1:
+                    store(c, 0, 2)
+                elif g > 1:
+                    store(c, g, g + 1)

@@ -19,7 +19,9 @@ ROWS = D // PACK
 W = 128
 CHUNKS = NQ // W
 UNITS = CHUNKS * H
-GROUPS = [(0, 1), (1, 2)] + [(u, u + 2) for u in range(2, UNITS - 2, 2)] + [(UNITS - 2, UNITS - 1), (UNITS - 1, UNITS)]
+ORDER = [(c, 0) for c in range(CHUNKS)] + [(c, g) for c in range(CHUNKS) for g in (2, 3, 1)]
+GROUPS = [(u, u + 1) for u in range(5)] + [(u, u + 2) for u in range(5, UNITS - 1, 2)] + [(UNITS - 1, UNITS)]
+I32 = mybir.dt.int32
 
 
 def tile_rows_a_relu_cap_kernel(tc, qT, kT, t, v, out):
@@ -31,15 +33,16 @@ def tile_rows_a_relu_cap_kernel(tc, qT, kT, t, v, out):
         def tiles(name, count, shape, dtype):
             return [sb.tile(shape, dtype, name="%s%d" % (name, i), align_bytes=64) for i in range(count)]
 
-        k_raw = tiles("k_raw", 2, [P, PACK, N // 2], F32)
+        k_raw = tiles("k_raw", 2, [ROWS, PACK, N // 2], F32)
         q_raw = tiles("q_raw", CHUNKS, [P, PACK, W], F32)
         v_raw = sb.tile([P, PACK, W], F32, align_bytes=64)
         t_sb = sb.tile([P, PACK], F32, align_bytes=64)
         k_bf = sb.tile([P, PACK, W, PACK], BF16, align_bytes=64)
         q_bf = tiles("q_bf", CHUNKS, [P, W, PACK], BF16)
         v_bf = sb.tile([P, W, PACK], BF16, align_bytes=64)
-        k_codes = tiles("k_codes", PACK, [P, W], U32)
-        k_scales = tiles("k_scales", PACK, [P, W], U8)
+        k_mx = sb.tile([P, N + N // 4], U32, align_bytes=64)
+        k_codes = k_mx[:, 0:N]
+        k_scales = k_mx[:, N : N + N // 4].bitcast(U8)
         q_codes = tiles("q_codes", CHUNKS, [P, W], U32)
         q_scales = tiles("q_scales", CHUNKS, [P, W], U8)
         v_codes = sb.tile([P, W], U32, align_bytes=64)
@@ -51,23 +54,20 @@ def tile_rows_a_relu_cap_kernel(tc, qT, kT, t, v, out):
         res = tiles("res", CHUNKS, [P, H, W], F32)
         warm_in = sb.tile([P, 1], F32, align_bytes=64)
         warm_out = sb.tile([P, 1], F32, align_bytes=64)
-        s_bank = [ps.tile([P, PACK, W], F32, name="s_bank%d" % g) for g in range(H)]
-        y_bank = [ps.tile([P, H, W], F32, name="y_bank%d" % g) for g in range(4)]
+        s_bank = [ps.tile([P, PACK, W], F32, name="s_bank%d" % g) for g in range(H + 2)]
+        y_bank = [ps.tile([P, H, W], F32, name="y_bank%d" % g) for g in range(2)]
 
         k_view = kT[0].rearrange("(p j) n -> p j n", j=PACK)
         q_view = qT.rearrange("h (p j) n -> (h p) j n", j=PACK)
 
-        def load_k(eng, half, g):
-            eng.dma_start(out=k_raw[half][ROWS * g : ROWS * (g + 1)], in_=k_view[:, :, 256 * half : 256 * (half + 1)])
-
-        def load_q(c):
-            nc.sync.dma_start(out=q_raw[c][:], in_=q_view[:, :, W * c : W * (c + 1)])
+        def load_q(eng, c):
+            eng.dma_start(out=q_raw[c][:], in_=q_view[:, :, W * c : W * (c + 1)])
 
         def deal_k(copy, s0, s1, r0):
             half = s0 // 64
             src = k_raw[half][:].rearrange("p j (s r) -> p s j r", r=PACK)
             src = src[:, s0 - 64 * half : s1 - 64 * half, :, r0 : r0 + 2]
-            copy(out=k_bf[:, r0 : r0 + 2, s0:s1, :].rearrange("p r s j -> p s j r"), in_=src)
+            copy(out=k_bf[0:ROWS, r0 : r0 + 2, s0:s1, :].rearrange("p r s j -> p s j r"), in_=src)
 
         def interleave(copy, dst, src):
             copy(out=dst[:].rearrange("p (c i) j -> p c j i", i=4), in_=src[:].rearrange("p j (c i) -> p c j i", i=4))
@@ -75,121 +75,116 @@ def tile_rows_a_relu_cap_kernel(tc, qT, kT, t, v, out):
         def quantize(codes, scales, src):
             nc.vector.quantize_mx(out=codes.bitcast(FP8X4), scales=scales, in_=src.rearrange("p c j -> p (c j)"))
 
-        def scores(u, r):
-            c, g = divmod(u, H)
+        def bank_of(u):
+            c, g = ORDER[u]
+            return (0, H, H + 1)[c % 3] if g == 0 else g
+
+        def scores(u):
+            c, g = ORDER[u]
             rows = slice(ROWS * g, ROWS * (g + 1))
-            nc.tensor.matmul_mx(
-                out=s_bank[g][:, r, :],
-                lhsT=k_codes[r][rows, :].bitcast(FP8X4),
-                lhsT_scale=k_scales[r][rows, :],
-                rhs=q_codes[c][rows, :].bitcast(FP8X4),
-                rhs_scale=q_scales[c][rows, :],
-                start=True,
-                stop=True,
+            for r in range(PACK):
+                nc.tensor.matmul_mx(
+                    out=s_bank[bank_of(u)][:, r, :],
+                    lhsT=k_codes[rows, W * r : W * (r + 1)].bitcast(FP8X4),
+                    lhsT_scale=k_scales[rows, W * r : W * (r + 1)],
+                    rhs=q_codes[c][rows, :].bitcast(FP8X4),
+                    rhs_scale=q_scales[c][rows, :],
+                    start=True,
+                    stop=True,
+                )
+
+        def weigh(u0, u1):
+            cols = slice(W * u0, W * u1)
+            t_rep = t_sb[:].unsqueeze(1).to_broadcast([P, W * (u1 - u0), PACK])
+            nc.vector.scalar_tensor_tensor(
+                out=w_bf[:, cols], in0=capped[:, cols], scalar=0.0, in1=t_rep, op0=ALU.max, op1=ALU.mult
             )
 
-        def y_slot(u):
-            c, g = divmod(u, H)
-            if c < CHUNKS - 1 or g < 2:
-                return y_bank[c]
-            return y_bank[g - 2]
+        def quantize_w(u0, u1):
+            cols = slice(W * u0, W * u1)
+            quantize(w_codes[:, cols], w_scales[:, cols], w_bf[:, cols])
 
-        def second(u):
-            g = u % H
-            nc.tensor.matmul_mx(
-                out=y_slot(u)[:, g, :],
-                lhsT=w_codes[:, W * u : W * (u + 1)].bitcast(FP8X4),
-                lhsT_scale=w_scales[:, W * u : W * (u + 1)],
-                rhs=v_codes[:].bitcast(FP8X4),
-                rhs_scale=v_scales[:],
-                start=True,
-                stop=True,
-            )
-
-        def store(c, g0, g1):
-            bank = y_slot(c * H + g0)
-            nc.scalar.activation(out=res[c][:, g0:g1, :], in_=bank[:, g0:g1, :], func=ACT.Copy, scale=0.125)
+        def finish(bank, c, g0, g1, on_vector=False):
+            for g in range(g0, g1):
+                u = ORDER.index((c, g))
+                nc.tensor.matmul_mx(
+                    out=bank[:, g, :],
+                    lhsT=w_codes[:, W * u : W * (u + 1)].bitcast(FP8X4),
+                    lhsT_scale=w_scales[:, W * u : W * (u + 1)],
+                    rhs=v_codes[:].bitcast(FP8X4),
+                    rhs_scale=v_scales[:],
+                    start=True,
+                    stop=True,
+                )
+            if on_vector:
+                nc.vector.tensor_scalar(
+                    out=res[c][:, g0:g1, :], in0=bank[:, g0:g1, :], scalar1=0.125, scalar2=None, op0=ALU.mult
+                )
+            else:
+                nc.scalar.activation(out=res[c][:, g0:g1, :], in_=bank[:, g0:g1, :], func=ACT.Copy, scale=0.125)
             nc.sync.dma_start(
                 out=out[g0:g1, W * c : W * (c + 1), :].rearrange("h p e -> p h e"), in_=res[c][:, g0:g1, :]
             )
 
         with tc.manual_schedule():
-            nc.gpsimd.dma_start(out=t_sb[:], in_=t.rearrange("(p j) o -> p (j o)", j=PACK))
-            load_q(0)
             for half in range(2):
-                for g in range(2):
-                    load_k(nc.sync, half, g)
-                    load_k(nc.scalar, half, g + 2)
-            load_q(1)
-            nc.sync.dma_start(out=v_raw[:], in_=v[0].rearrange("(p j) e -> p j e", j=PACK))
-            load_q(2)
-            load_q(3)
+                nc.sync.dma_start(out=k_raw[half][:], in_=k_view[:, :, 256 * half : 256 * (half + 1)])
+            load_q(nc.scalar, 0)
+            for c in range(1, CHUNKS):
+                load_q(nc.sync, c)
+            nc.sync.dma_start(out=t_sb[:], in_=t.rearrange("(p j) o -> p (j o)", j=PACK))
 
             nc.vector.memset(warm_in[:], 0.0)
             nc.scalar.activation(out=warm_out[:], in_=warm_in[:], func=ACT.Tanh, scale=0.5)
+            nc.vector.memset(k_bf[:].rearrange("p r s j -> p (r s j)").bitcast(U32), 0)
+            nc.vector.memset(k_mx[:, N : N + N // 4], 0)
 
-            interleave(nc.vector.tensor_copy, q_bf[0], q_raw[0])
-            quantize(q_codes[0][:], q_scales[0][:], q_bf[0][:])
             for half in range(2):
                 s0 = 64 * half
                 deal_k(nc.vector.tensor_copy, s0, s0 + 64, 0)
                 deal_k(nc.vector.tensor_copy, s0, s0 + 32, 2)
                 deal_k(nc.scalar.copy, s0 + 32, s0 + 64, 2)
+                if half == 0:
+                    interleave(nc.scalar.copy, q_bf[0], q_raw[0])
+                else:
+                    quantize(q_codes[0][:], q_scales[0][:], q_bf[0][:])
                 for r in range(PACK):
-                    quantize(k_codes[r][:, s0 : s0 + 64], k_scales[r][:, s0 : s0 + 64], k_bf[:, r, s0 : s0 + 64])
-            for g in range(H):
-                for r in range(PACK):
-                    scores(g, r)
+                    cols = slice(W * r + s0, W * r + s0 + 64)
+                    quantize(k_codes[:, cols], k_scales[:, cols], k_bf[:, r, s0 : s0 + 64])
+            for g in (2, 3, 1):
+                nc.sync.dma_start(out=k_mx[ROWS * g : ROWS * (g + 1), :].bitcast(I32), in_=k_mx[0:ROWS, :].bitcast(I32))
+            nc.sync.dma_start(out=v_raw[:], in_=v[0].rearrange("(p j) e -> p j e", j=PACK))
             interleave(nc.scalar.copy, q_bf[1], q_raw[1])
-            interleave(nc.vector.tensor_copy, v_bf, v_raw)
             quantize(q_codes[1][:], q_scales[1][:], q_bf[1][:])
-            quantize(v_codes[:], v_scales[:], v_bf[:])
-            interleave(nc.vector.tensor_copy, q_bf[2], q_raw[2])
-
-            def weigh(u0, u1):
-                cols = slice(W * u0, W * u1)
-                t_rep = t_sb[:].unsqueeze(1).to_broadcast([P, W * (u1 - u0), PACK])
-                nc.vector.scalar_tensor_tensor(
-                    out=w_bf[:, cols], in0=capped[:, cols], scalar=0.0, in1=t_rep, op0=ALU.max, op1=ALU.mult
-                )
-
-            def quantize_w(u0, u1):
-                cols = slice(W * u0, W * u1)
-                quantize(w_codes[:, cols], w_scales[:, cols], w_bf[:, cols])
+            interleave(nc.scalar.copy, q_bf[2], q_raw[2])
+            interleave(nc.vector.tensor_copy, q_bf[3], q_raw[3])
+            quantize(q_codes[2][:], q_scales[2][:], q_bf[2][:])
+            quantize(q_codes[3][:], q_scales[3][:], q_bf[3][:])
 
             group_ending = {u1 - 1: i for i, (u0, u1) in enumerate(GROUPS)}
+            issued = 0
             for s in range(UNITS):
-                if s < UNITS:
-                    nc.scalar.activation(
-                        out=capped[:, W * s : W * (s + 1)],
-                        in_=s_bank[s % H][:].rearrange("p r q -> p q r"),
-                        func=ACT.Tanh,
-                        scale=0.5,
-                    )
-                if s + H < UNITS:
-                    for r in range(PACK):
-                        scores(s + H, r)
+                while issued < UNITS and all(bank_of(u) != bank_of(issued) for u in range(s, issued)):
+                    scores(issued)
+                    issued += 1
+                nc.scalar.activation(
+                    out=capped[:, W * s : W * (s + 1)],
+                    in_=s_bank[bank_of(s)][:].rearrange("p r q -> p q r"),
+                    func=ACT.Tanh,
+                    scale=0.5,
+                )
                 if s in group_ending:
                     i = group_ending[s]
                     weigh(*GROUPS[i])
-                    if i == 0:
-                        quantize(q_codes[2][:], q_scales[2][:], q_bf[2][:])
-                    elif i == 1:
-                        quantize_w(*GROUPS[0])
-                        quantize_w(*GROUPS[1])
-                    elif i > 2:
+                    if i > 0:
                         quantize_w(*GROUPS[i - 1])
-                if s == 7:
-                    interleave(nc.scalar.copy, q_bf[3], q_raw[3])
-                    quantize(q_codes[3][:], q_scales[3][:], q_bf[3][:])
+                if s == 10:
+                    interleave(nc.scalar.copy, v_bf, v_raw)
+                    quantize(v_codes[:], v_scales[:], v_bf[:])
             quantize_w(*GROUPS[-1])
-            for u in range(UNITS):
-                second(u)
-                c, g = divmod(u, H)
-                if c < CHUNKS - 1:
-                    if g == H - 1:
-                        store(c, 0, H)
-                elif g == 1:
-                    store(c, 0, 2)
-                elif g > 1:
-                    store(c, g, g + 1)
+            finish(y_bank[0], 0, 0, H)
+            finish(y_bank[1], 1, 0, H)
+            finish(y_bank[0], 3, 0, 1)
+            finish(y_bank[1], 2, 0, H)
+            finish(y_bank[0], 3, 2, H)
+            finish(y_bank[1], 3, 1, 2, on_vector=True)

@@ -20,7 +20,18 @@ W = 128
 CHUNKS = NQ // W
 UNITS = CHUNKS * H
 ORDER = [(c, 0) for c in range(CHUNKS)] + [(c, g) for c in range(CHUNKS) for g in (2, 3, 1)]
-GROUPS = [(u, u + 1) for u in range(5)] + [(u, u + 2) for u in range(5, UNITS - 1, 2)] + [(UNITS - 1, UNITS)]
+VECTOR_PLAN = {
+    0: [("w", 0, 1)],
+    1: [("w", 1, 2), ("q", 0, 1), ("q", 1, 2)],
+    3: [("w", 2, 4)],
+    5: [("w", 4, 6)],
+    7: [("w", 6, 8), ("q", 2, 6)],
+    9: [("w", 8, 10)],
+    11: [("w", 10, 12), ("q", 6, 10)],
+    13: [("w", 12, 14), ("q", 10, 12)],
+    14: [("w", 14, 15), ("q", 12, 14)],
+    15: [("w", 15, 16), ("q", 14, 15), ("q", 15, 16)],
+}
 I32 = mybir.dt.int32
 
 
@@ -51,7 +62,7 @@ def tile_rows_a_relu_cap_kernel(tc, qT, kT, t, v, out):
         w_bf = sb.tile([P, UNITS * W, PACK], BF16, align_bytes=64)
         w_codes = sb.tile([P, UNITS * W], U32, align_bytes=64)
         w_scales = sb.tile([P, UNITS * W], U8, align_bytes=64)
-        res = tiles("res", CHUNKS, [P, H, W], F32)
+        res = sb.tile([P, UNITS, W], F32, align_bytes=64)
         warm_in = sb.tile([P, 1], F32, align_bytes=64)
         warm_out = sb.tile([P, 1], F32, align_bytes=64)
         s_bank = [ps.tile([P, PACK, W], F32, name="s_bank%d" % g) for g in range(H + 2)]
@@ -104,11 +115,12 @@ def tile_rows_a_relu_cap_kernel(tc, qT, kT, t, v, out):
             cols = slice(W * u0, W * u1)
             quantize(w_codes[:, cols], w_scales[:, cols], w_bf[:, cols])
 
-        def finish(bank, c, g0, g1, on_vector=False):
-            for g in range(g0, g1):
-                u = ORDER.index((c, g))
+        def finish(bank, u0, u1, on_vector=False):
+            c, g = min(ORDER[u0:u1])
+            for u in range(u0, u1):
+                i = sorted(ORDER[u0:u1]).index(ORDER[u])
                 nc.tensor.matmul_mx(
-                    out=bank[:, g, :],
+                    out=bank[:, i, :],
                     lhsT=w_codes[:, W * u : W * (u + 1)].bitcast(FP8X4),
                     lhsT_scale=w_scales[:, W * u : W * (u + 1)],
                     rhs=v_codes[:].bitcast(FP8X4),
@@ -116,15 +128,18 @@ def tile_rows_a_relu_cap_kernel(tc, qT, kT, t, v, out):
                     start=True,
                     stop=True,
                 )
+            n = u1 - u0
             if on_vector:
                 nc.vector.tensor_scalar(
-                    out=res[c][:, g0:g1, :], in0=bank[:, g0:g1, :], scalar1=0.125, scalar2=None, op0=ALU.mult
+                    out=res[:, u0:u1, :], in0=bank[:, 0:n, :], scalar1=0.125, scalar2=None, op0=ALU.mult
                 )
             else:
-                nc.scalar.activation(out=res[c][:, g0:g1, :], in_=bank[:, g0:g1, :], func=ACT.Copy, scale=0.125)
-            nc.sync.dma_start(
-                out=out[g0:g1, W * c : W * (c + 1), :].rearrange("h p e -> p h e"), in_=res[c][:, g0:g1, :]
-            )
+                nc.scalar.activation(out=res[:, u0:u1, :], in_=bank[:, 0:n, :], func=ACT.Copy, scale=0.125)
+            if g == 0:
+                dst = out[0].rearrange("(c p) e -> p c e", p=W)
+            else:
+                dst = out[g : g + n, W * c : W * (c + 1), :].rearrange("h p e -> p h e")
+            nc.sync.dma_start(out=dst, in_=res[:, u0:u1, :])
 
         with tc.manual_schedule():
             for half in range(2):
@@ -133,6 +148,7 @@ def tile_rows_a_relu_cap_kernel(tc, qT, kT, t, v, out):
             for c in range(1, CHUNKS):
                 load_q(nc.sync, c)
             nc.sync.dma_start(out=t_sb[:], in_=t.rearrange("(p j) o -> p (j o)", j=PACK))
+            nc.sync.dma_start(out=v_raw[:], in_=v[0].rearrange("(p j) e -> p j e", j=PACK))
 
             nc.vector.memset(warm_in[:], 0.0)
             nc.scalar.activation(out=warm_out[:], in_=warm_in[:], func=ACT.Tanh, scale=0.5)
@@ -153,15 +169,14 @@ def tile_rows_a_relu_cap_kernel(tc, qT, kT, t, v, out):
                     quantize(k_codes[:, cols], k_scales[:, cols], k_bf[:, r, s0 : s0 + 64])
             for g in (2, 3, 1):
                 nc.sync.dma_start(out=k_mx[ROWS * g : ROWS * (g + 1), :].bitcast(I32), in_=k_mx[0:ROWS, :].bitcast(I32))
-            nc.sync.dma_start(out=v_raw[:], in_=v[0].rearrange("(p j) e -> p j e", j=PACK))
             interleave(nc.scalar.copy, q_bf[1], q_raw[1])
             quantize(q_codes[1][:], q_scales[1][:], q_bf[1][:])
             interleave(nc.scalar.copy, q_bf[2], q_raw[2])
             interleave(nc.vector.tensor_copy, q_bf[3], q_raw[3])
             quantize(q_codes[2][:], q_scales[2][:], q_bf[2][:])
             quantize(q_codes[3][:], q_scales[3][:], q_bf[3][:])
+            interleave(nc.vector.tensor_copy, v_bf, v_raw)
 
-            group_ending = {u1 - 1: i for i, (u0, u1) in enumerate(GROUPS)}
             issued = 0
             for s in range(UNITS):
                 while issued < UNITS and all(bank_of(u) != bank_of(issued) for u in range(s, issued)):
@@ -173,18 +188,13 @@ def tile_rows_a_relu_cap_kernel(tc, qT, kT, t, v, out):
                     func=ACT.Tanh,
                     scale=0.5,
                 )
-                if s in group_ending:
-                    i = group_ending[s]
-                    weigh(*GROUPS[i])
-                    if i > 0:
-                        quantize_w(*GROUPS[i - 1])
-                if s == 10:
-                    interleave(nc.scalar.copy, v_bf, v_raw)
+                for step, u0, u1 in VECTOR_PLAN.get(s, []):
+                    (weigh if step == "w" else quantize_w)(u0, u1)
+                if s == 0:
                     quantize(v_codes[:], v_scales[:], v_bf[:])
-            quantize_w(*GROUPS[-1])
-            finish(y_bank[0], 0, 0, H)
-            finish(y_bank[1], 1, 0, H)
-            finish(y_bank[0], 3, 0, 1)
-            finish(y_bank[1], 2, 0, H)
-            finish(y_bank[0], 3, 2, H)
-            finish(y_bank[1], 3, 1, 2, on_vector=True)
+            finish(y_bank[0], 0, 4)
+            finish(y_bank[1], 4, 7)
+            finish(y_bank[0], 7, 10)
+            finish(y_bank[1], 10, 13)
+            finish(y_bank[0], 13, 15)
+            finish(y_bank[1], 15, 16, on_vector=True)

@@ -7,6 +7,7 @@ FLOPS = 2 * 2 * H * NQ * N * D
 
 F32 = mybir.dt.float32
 BF16 = mybir.dt.bfloat16
+I32 = mybir.dt.int32
 U32 = mybir.dt.uint32
 U8 = mybir.dt.uint8
 FP8X4 = mybir.dt.float8_e4m3fn_x4
@@ -17,22 +18,31 @@ P = 128
 PACK = 4
 ROWS = D // PACK
 W = 128
+HALF = W // 2
 CHUNKS = NQ // W
 UNITS = CHUNKS * H
-ORDER = [(c, 0) for c in range(CHUNKS)] + [(c, g) for c in range(CHUNKS) for g in (2, 3, 1)]
+SCALE_WORDS = N // 4
+OUT_SCALE = 2.0 / 16.0
+HEAD0_BANKS = 3
+COPY_ORDER = (2, 3, 1)
+
+ORDER = [(0, 0), (1, 0), (2, 0)] + [(0, g) for g in COPY_ORDER] + [(3, 0)]
+ORDER = ORDER + [(c, g) for c in range(1, CHUNKS) for g in COPY_ORDER]
+RUNS = [[0, 1, 2, 6], [3, 4, 5], [7, 8, 9], [10, 11, 12], [13, 14], [15]]
 VECTOR_PLAN = {
     0: [("w", 0, 1)],
-    1: [("w", 1, 2), ("q", 0, 1), ("q", 1, 2)],
-    3: [("w", 2, 4)],
-    5: [("w", 4, 6)],
-    7: [("w", 6, 8), ("q", 2, 6)],
-    9: [("w", 8, 10)],
-    11: [("w", 10, 12), ("q", 6, 10)],
-    13: [("w", 12, 14), ("q", 10, 12)],
-    14: [("w", 14, 15), ("q", 12, 14)],
+    1: [("w", 1, 2)],
+    2: [("w", 2, 3), ("q", 0, 2)],
+    3: [("w", 3, 4)],
+    4: [("w", 4, 5), ("q", 2, 4)],
+    5: [("w", 5, 6)],
+    7: [("w", 6, 8)],
+    9: [("w", 8, 10), ("q", 4, 8)],
+    11: [("w", 10, 12)],
+    13: [("w", 12, 14), ("q", 8, 12), ("q", 12, 14)],
+    14: [("w", 14, 15)],
     15: [("w", 15, 16), ("q", 14, 15), ("q", 15, 16)],
 }
-I32 = mybir.dt.int32
 
 
 def tile_rows_a_relu_cap_kernel(tc, qT, kT, t, v, out):
@@ -51,9 +61,9 @@ def tile_rows_a_relu_cap_kernel(tc, qT, kT, t, v, out):
         k_bf = sb.tile([P, PACK, W, PACK], BF16, align_bytes=64)
         q_bf = tiles("q_bf", CHUNKS, [P, W, PACK], BF16)
         v_bf = sb.tile([P, W, PACK], BF16, align_bytes=64)
-        k_mx = sb.tile([P, N + N // 4], U32, align_bytes=64)
+        k_mx = sb.tile([P, N + SCALE_WORDS], U32, align_bytes=64)
         k_codes = k_mx[:, 0:N]
-        k_scales = k_mx[:, N : N + N // 4].bitcast(U8)
+        k_scales = k_mx[:, N : N + SCALE_WORDS].bitcast(U8)
         q_codes = tiles("q_codes", CHUNKS, [P, W], U32)
         q_scales = tiles("q_scales", CHUNKS, [P, W], U8)
         v_codes = sb.tile([P, W], U32, align_bytes=64)
@@ -65,7 +75,7 @@ def tile_rows_a_relu_cap_kernel(tc, qT, kT, t, v, out):
         res = sb.tile([P, UNITS, W], F32, align_bytes=64)
         warm_in = sb.tile([P, 1], F32, align_bytes=64)
         warm_out = sb.tile([P, 1], F32, align_bytes=64)
-        s_bank = [ps.tile([P, PACK, W], F32, name="s_bank%d" % g) for g in range(H + 2)]
+        s_bank = [ps.tile([P, PACK, W], F32, name="s_bank%d" % g) for g in range(H + HEAD0_BANKS - 1)]
         y_bank = [ps.tile([P, H, W], F32, name="y_bank%d" % g) for g in range(2)]
 
         k_view = kT[0].rearrange("(p j) n -> p j n", j=PACK)
@@ -75,9 +85,9 @@ def tile_rows_a_relu_cap_kernel(tc, qT, kT, t, v, out):
             eng.dma_start(out=q_raw[c][:], in_=q_view[:, :, W * c : W * (c + 1)])
 
         def deal_k(copy, s0, s1, r0):
-            half = s0 // 64
+            half = s0 // HALF
             src = k_raw[half][:].rearrange("p j (s r) -> p s j r", r=PACK)
-            src = src[:, s0 - 64 * half : s1 - 64 * half, :, r0 : r0 + 2]
+            src = src[:, s0 - HALF * half : s1 - HALF * half, :, r0 : r0 + 2]
             copy(out=k_bf[0:ROWS, r0 : r0 + 2, s0:s1, :].rearrange("p r s j -> p s j r"), in_=src)
 
         def interleave(copy, dst, src):
@@ -86,9 +96,12 @@ def tile_rows_a_relu_cap_kernel(tc, qT, kT, t, v, out):
         def quantize(codes, scales, src):
             nc.vector.quantize_mx(out=codes.bitcast(FP8X4), scales=scales, in_=src.rearrange("p c j -> p (c j)"))
 
+        def quantize_q(c):
+            quantize(q_codes[c][:], q_scales[c][:], q_bf[c][:])
+
         def bank_of(u):
             c, g = ORDER[u]
-            return (0, H, H + 1)[c % 3] if g == 0 else g
+            return (0, H, H + 1)[c % HEAD0_BANKS] if g == 0 else g
 
         def scores(u):
             c, g = ORDER[u]
@@ -115,12 +128,13 @@ def tile_rows_a_relu_cap_kernel(tc, qT, kT, t, v, out):
             cols = slice(W * u0, W * u1)
             quantize(w_codes[:, cols], w_scales[:, cols], w_bf[:, cols])
 
-        def finish(bank, u0, u1, on_vector=False):
-            c, g = min(ORDER[u0:u1])
-            for u in range(u0, u1):
-                i = sorted(ORDER[u0:u1]).index(ORDER[u])
+        def finish(bank, first, units, on_vector):
+            places = sorted(ORDER[u] for u in units)
+            c, g = places[0]
+            n = len(units)
+            for u in units:
                 nc.tensor.matmul_mx(
-                    out=bank[:, i, :],
+                    out=bank[:, places.index(ORDER[u]), :],
                     lhsT=w_codes[:, W * u : W * (u + 1)].bitcast(FP8X4),
                     lhsT_scale=w_scales[:, W * u : W * (u + 1)],
                     rhs=v_codes[:].bitcast(FP8X4),
@@ -128,22 +142,20 @@ def tile_rows_a_relu_cap_kernel(tc, qT, kT, t, v, out):
                     start=True,
                     stop=True,
                 )
-            n = u1 - u0
+            staged = res[:, first : first + n, :]
             if on_vector:
-                nc.vector.tensor_scalar(
-                    out=res[:, u0:u1, :], in0=bank[:, 0:n, :], scalar1=0.125, scalar2=None, op0=ALU.mult
-                )
+                nc.vector.tensor_scalar(out=staged, in0=bank[:, 0:n, :], scalar1=OUT_SCALE, scalar2=None, op0=ALU.mult)
             else:
-                nc.scalar.activation(out=res[:, u0:u1, :], in_=bank[:, 0:n, :], func=ACT.Copy, scale=0.125)
+                nc.scalar.activation(out=staged, in_=bank[:, 0:n, :], func=ACT.Copy, scale=OUT_SCALE)
             if g == 0:
                 dst = out[0].rearrange("(c p) e -> p c e", p=W)
             else:
                 dst = out[g : g + n, W * c : W * (c + 1), :].rearrange("h p e -> p h e")
-            nc.sync.dma_start(out=dst, in_=res[:, u0:u1, :])
+            nc.sync.dma_start(out=dst, in_=staged)
 
         with tc.manual_schedule():
             for half in range(2):
-                nc.sync.dma_start(out=k_raw[half][:], in_=k_view[:, :, 256 * half : 256 * (half + 1)])
+                nc.sync.dma_start(out=k_raw[half][:], in_=k_view[:, :, N // 2 * half : N // 2 * (half + 1)])
             load_q(nc.scalar, 0)
             for c in range(1, CHUNKS):
                 load_q(nc.sync, c)
@@ -153,29 +165,27 @@ def tile_rows_a_relu_cap_kernel(tc, qT, kT, t, v, out):
             nc.vector.memset(warm_in[:], 0.0)
             nc.scalar.activation(out=warm_out[:], in_=warm_in[:], func=ACT.Tanh, scale=0.5)
             nc.vector.memset(k_bf[:].rearrange("p r s j -> p (r s j)").bitcast(U32), 0)
-            nc.vector.memset(k_mx[:, N : N + N // 4], 0)
+            nc.vector.memset(k_mx[:, N : N + SCALE_WORDS], 0)
 
             for half in range(2):
-                s0 = 64 * half
-                deal_k(nc.vector.tensor_copy, s0, s0 + 64, 0)
-                deal_k(nc.vector.tensor_copy, s0, s0 + 32, 2)
-                deal_k(nc.scalar.copy, s0 + 32, s0 + 64, 2)
+                s0 = HALF * half
+                deal_k(nc.vector.tensor_copy, s0, s0 + HALF, 0)
+                deal_k(nc.vector.tensor_copy, s0, s0 + HALF // 2, 2)
+                deal_k(nc.scalar.copy, s0 + HALF // 2, s0 + HALF, 2)
                 if half == 0:
                     interleave(nc.scalar.copy, q_bf[0], q_raw[0])
                 else:
-                    quantize(q_codes[0][:], q_scales[0][:], q_bf[0][:])
+                    quantize_q(0)
                 for r in range(PACK):
-                    cols = slice(W * r + s0, W * r + s0 + 64)
-                    quantize(k_codes[:, cols], k_scales[:, cols], k_bf[:, r, s0 : s0 + 64])
-            for g in (2, 3, 1):
+                    cols = slice(W * r + s0, W * r + s0 + HALF)
+                    quantize(k_codes[:, cols], k_scales[:, cols], k_bf[:, r, s0 : s0 + HALF])
+            for g in COPY_ORDER:
                 nc.sync.dma_start(out=k_mx[ROWS * g : ROWS * (g + 1), :].bitcast(I32), in_=k_mx[0:ROWS, :].bitcast(I32))
             interleave(nc.scalar.copy, q_bf[1], q_raw[1])
-            quantize(q_codes[1][:], q_scales[1][:], q_bf[1][:])
-            interleave(nc.scalar.copy, q_bf[2], q_raw[2])
+            quantize_q(1)
+            interleave(nc.vector.tensor_copy, q_bf[2], q_raw[2])
+            quantize_q(2)
             interleave(nc.vector.tensor_copy, q_bf[3], q_raw[3])
-            quantize(q_codes[2][:], q_scales[2][:], q_bf[2][:])
-            quantize(q_codes[3][:], q_scales[3][:], q_bf[3][:])
-            interleave(nc.vector.tensor_copy, v_bf, v_raw)
 
             issued = 0
             for s in range(UNITS):
@@ -190,11 +200,14 @@ def tile_rows_a_relu_cap_kernel(tc, qT, kT, t, v, out):
                 )
                 for step, u0, u1 in VECTOR_PLAN.get(s, []):
                     (weigh if step == "w" else quantize_w)(u0, u1)
-                if s == 0:
-                    quantize(v_codes[:], v_scales[:], v_bf[:])
-            finish(y_bank[0], 0, 4)
-            finish(y_bank[1], 4, 7)
-            finish(y_bank[0], 7, 10)
-            finish(y_bank[1], 10, 13)
-            finish(y_bank[0], 13, 15)
-            finish(y_bank[1], 15, 16, on_vector=True)
+                    if (step, u0) == ("w", 0):
+                        quantize_q(CHUNKS - 1)
+                    if (step, u0) == ("w", 1):
+                        interleave(nc.vector.tensor_copy, v_bf, v_raw)
+                    if (step, u0) == ("w", 2):
+                        quantize(v_codes[:], v_scales[:], v_bf[:])
+
+            first = 0
+            for i, units in enumerate(RUNS):
+                finish(y_bank[i % 2], first, units, on_vector=i == len(RUNS) - 1)
+                first += len(units)

from contextlib import ExitStack

import concourse.mybir as mybir

H, D, NQ, N = 4, 128, 512, 512
FLOPS = 2 * 2 * H * NQ * N * D

F32 = mybir.dt.float32
BF16 = mybir.dt.bfloat16
I32 = mybir.dt.int32
U32 = mybir.dt.uint32
U8 = mybir.dt.uint8
FP8X4 = mybir.dt.float8_e4m3fn_x4
ACT = mybir.ActivationFunctionType
ALU = mybir.AluOpType

P = 128
PACK = 4
ROWS = D // PACK
W = 128
HALF = W // 2
CHUNKS = NQ // W
UNITS = CHUNKS * H
SCALE_WORDS = N // 4
OUT_SCALE = 2.0 / 16.0
HEAD0_BANKS = 3
COPY_ORDER = (2, 3, 1)

ORDER = [(0, 0), (1, 0), (2, 0)] + [(0, g) for g in COPY_ORDER] + [(3, 0)]
ORDER = ORDER + [(c, g) for c in range(1, CHUNKS) for g in COPY_ORDER]
RUNS = [[0, 1, 2, 6], [3, 4, 5], [7, 8, 9], [10, 11, 12], [13, 14], [15]]
VECTOR_PLAN = {
    0: [("w", 0, 1)],
    1: [("w", 1, 2)],
    2: [("w", 2, 3), ("q", 0, 2)],
    3: [("w", 3, 4)],
    4: [("w", 4, 5), ("q", 2, 4)],
    5: [("w", 5, 6)],
    7: [("w", 6, 8)],
    9: [("w", 8, 10), ("q", 4, 8)],
    11: [("w", 10, 12)],
    13: [("w", 12, 14), ("q", 8, 12), ("q", 12, 14)],
    14: [("w", 14, 15)],
    15: [("w", 15, 16), ("q", 14, 15), ("q", 15, 16)],
}


def tile_rows_a_relu_cap_kernel(tc, qT, kT, t, v, out):
    nc = tc.nc
    with ExitStack() as ctx:
        sb = ctx.enter_context(tc.tile_pool(name="sb", bufs=1))
        ps = ctx.enter_context(tc.psum_pool(name="ps", bufs=1))

        def tiles(name, count, shape, dtype):
            return [sb.tile(shape, dtype, name="%s%d" % (name, i), align_bytes=64) for i in range(count)]

        k_raw = tiles("k_raw", 2, [ROWS, PACK, N // 2], F32)
        q_raw = tiles("q_raw", CHUNKS, [P, PACK, W], F32)
        v_raw = sb.tile([P, PACK, W], F32, align_bytes=64)
        t_sb = sb.tile([P, PACK], F32, align_bytes=64)
        k_bf = sb.tile([P, PACK, W, PACK], BF16, align_bytes=64)
        q_bf = tiles("q_bf", CHUNKS, [P, W, PACK], BF16)
        v_bf = sb.tile([P, W, PACK], BF16, align_bytes=64)
        k_mx = sb.tile([P, N + SCALE_WORDS], U32, align_bytes=64)
        k_codes = k_mx[:, 0:N]
        k_scales = k_mx[:, N : N + SCALE_WORDS].bitcast(U8)
        q_codes = tiles("q_codes", CHUNKS, [P, W], U32)
        q_scales = tiles("q_scales", CHUNKS, [P, W], U8)
        v_codes = sb.tile([P, W], U32, align_bytes=64)
        v_scales = sb.tile([P, W], U8, align_bytes=64)
        capped = sb.tile([P, UNITS * W, PACK], F32, align_bytes=64)
        w_bf = sb.tile([P, UNITS * W, PACK], BF16, align_bytes=64)
        w_codes = sb.tile([P, UNITS * W], U32, align_bytes=64)
        w_scales = sb.tile([P, UNITS * W], U8, align_bytes=64)
        res = sb.tile([P, UNITS, W], F32, align_bytes=64)
        warm_in = sb.tile([P, 1], F32, align_bytes=64)
        warm_out = sb.tile([P, 1], F32, align_bytes=64)
        s_bank = [ps.tile([P, PACK, W], F32, name="s_bank%d" % g) for g in range(H + HEAD0_BANKS - 1)]
        y_bank = [ps.tile([P, H, W], F32, name="y_bank%d" % g) for g in range(2)]

        k_view = kT[0].rearrange("(p j) n -> p j n", j=PACK)
        q_view = qT.rearrange("h (p j) n -> (h p) j n", j=PACK)

        def load_q(eng, c):
            eng.dma_start(out=q_raw[c][:], in_=q_view[:, :, W * c : W * (c + 1)])

        def deal_k(copy, s0, s1, r0):
            half = s0 // HALF
            src = k_raw[half][:].rearrange("p j (s r) -> p s j r", r=PACK)
            src = src[:, s0 - HALF * half : s1 - HALF * half, :, r0 : r0 + 2]
            copy(out=k_bf[0:ROWS, r0 : r0 + 2, s0:s1, :].rearrange("p r s j -> p s j r"), in_=src)

        def interleave(copy, dst, src):
            copy(out=dst[:].rearrange("p (c i) j -> p c j i", i=4), in_=src[:].rearrange("p j (c i) -> p c j i", i=4))

        def quantize(codes, scales, src):
            nc.vector.quantize_mx(out=codes.bitcast(FP8X4), scales=scales, in_=src.rearrange("p c j -> p (c j)"))

        def quantize_q(c):
            quantize(q_codes[c][:], q_scales[c][:], q_bf[c][:])

        def bank_of(u):
            c, g = ORDER[u]
            return (0, H, H + 1)[c % HEAD0_BANKS] if g == 0 else g

        def scores(u):
            c, g = ORDER[u]
            rows = slice(ROWS * g, ROWS * (g + 1))
            for r in range(PACK):
                nc.tensor.matmul_mx(
                    out=s_bank[bank_of(u)][:, r, :],
                    lhsT=k_codes[rows, W * r : W * (r + 1)].bitcast(FP8X4),
                    lhsT_scale=k_scales[rows, W * r : W * (r + 1)],
                    rhs=q_codes[c][rows, :].bitcast(FP8X4),
                    rhs_scale=q_scales[c][rows, :],
                    start=True,
                    stop=True,
                )

        def weigh(u0, u1):
            cols = slice(W * u0, W * u1)
            t_rep = t_sb[:].unsqueeze(1).to_broadcast([P, W * (u1 - u0), PACK])
            nc.vector.scalar_tensor_tensor(
                out=w_bf[:, cols], in0=capped[:, cols], scalar=0.0, in1=t_rep, op0=ALU.max, op1=ALU.mult
            )

        def quantize_w(u0, u1):
            cols = slice(W * u0, W * u1)
            quantize(w_codes[:, cols], w_scales[:, cols], w_bf[:, cols])

        def finish(bank, first, units, on_vector):
            places = sorted(ORDER[u] for u in units)
            c, g = places[0]
            n = len(units)
            for u in units:
                nc.tensor.matmul_mx(
                    out=bank[:, places.index(ORDER[u]), :],
                    lhsT=w_codes[:, W * u : W * (u + 1)].bitcast(FP8X4),
                    lhsT_scale=w_scales[:, W * u : W * (u + 1)],
                    rhs=v_codes[:].bitcast(FP8X4),
                    rhs_scale=v_scales[:],
                    start=True,
                    stop=True,
                )
            staged = res[:, first : first + n, :]
            if on_vector:
                nc.vector.tensor_scalar(out=staged, in0=bank[:, 0:n, :], scalar1=OUT_SCALE, scalar2=None, op0=ALU.mult)
            else:
                nc.scalar.activation(out=staged, in_=bank[:, 0:n, :], func=ACT.Copy, scale=OUT_SCALE)
            if g == 0:
                dst = out[0].rearrange("(c p) e -> p c e", p=W)
            else:
                dst = out[g : g + n, W * c : W * (c + 1), :].rearrange("h p e -> p h e")
            nc.sync.dma_start(out=dst, in_=staged)

        with tc.manual_schedule():
            for half in range(2):
                nc.sync.dma_start(out=k_raw[half][:], in_=k_view[:, :, N // 2 * half : N // 2 * (half + 1)])
            load_q(nc.scalar, 0)
            for c in range(1, CHUNKS):
                load_q(nc.sync, c)
            nc.sync.dma_start(out=t_sb[:], in_=t.rearrange("(p j) o -> p (j o)", j=PACK))
            nc.sync.dma_start(out=v_raw[:], in_=v[0].rearrange("(p j) e -> p j e", j=PACK))

            nc.vector.memset(warm_in[:], 0.0)
            nc.scalar.activation(out=warm_out[:], in_=warm_in[:], func=ACT.Tanh, scale=0.5)
            nc.vector.memset(k_bf[:].rearrange("p r s j -> p (r s j)").bitcast(U32), 0)
            nc.vector.memset(k_mx[:, N : N + SCALE_WORDS], 0)

            for half in range(2):
                s0 = HALF * half
                deal_k(nc.vector.tensor_copy, s0, s0 + HALF, 0)
                deal_k(nc.vector.tensor_copy, s0, s0 + HALF // 2, 2)
                deal_k(nc.scalar.copy, s0 + HALF // 2, s0 + HALF, 2)
                if half == 0:
                    interleave(nc.scalar.copy, q_bf[0], q_raw[0])
                else:
                    quantize_q(0)
                for r in range(PACK):
                    cols = slice(W * r + s0, W * r + s0 + HALF)
                    quantize(k_codes[:, cols], k_scales[:, cols], k_bf[:, r, s0 : s0 + HALF])
            for g in COPY_ORDER:
                nc.sync.dma_start(out=k_mx[ROWS * g : ROWS * (g + 1), :].bitcast(I32), in_=k_mx[0:ROWS, :].bitcast(I32))
            interleave(nc.scalar.copy, q_bf[1], q_raw[1])
            quantize_q(1)
            interleave(nc.vector.tensor_copy, q_bf[2], q_raw[2])
            quantize_q(2)
            interleave(nc.vector.tensor_copy, q_bf[3], q_raw[3])

            issued = 0
            for s in range(UNITS):
                while issued < UNITS and all(bank_of(u) != bank_of(issued) for u in range(s, issued)):
                    scores(issued)
                    issued += 1
                nc.scalar.activation(
                    out=capped[:, W * s : W * (s + 1)],
                    in_=s_bank[bank_of(s)][:].rearrange("p r q -> p q r"),
                    func=ACT.Tanh,
                    scale=0.5,
                )
                for step, u0, u1 in VECTOR_PLAN.get(s, []):
                    (weigh if step == "w" else quantize_w)(u0, u1)
                    if (step, u0) == ("w", 0):
                        quantize_q(CHUNKS - 1)
                    if (step, u0) == ("w", 1):
                        interleave(nc.vector.tensor_copy, v_bf, v_raw)
                    if (step, u0) == ("w", 2):
                        quantize(v_codes[:], v_scales[:], v_bf[:])

            first = 0
            for i, units in enumerate(RUNS):
                finish(y_bank[i % 2], first, units, on_vector=i == len(RUNS) - 1)
                first += len(units)
